import numpy as np, ml_dtypes
CORES = [9,25,41,57]
N = 4
import mx_ref
BF = ml_dtypes.bfloat16
def gentries(a):
    return np.ascontiguousarray(a.reshape(8, 16, -1).transpose(0, 2, 1)).reshape(8, -1)
def gtable(e):
    e = np.asarray(e); return np.ascontiguousarray(e.reshape(8, -1, 16).transpose(0, 2, 1)).reshape(128, -1).astype(np.int32)
def gcols(t, e):
    v = np.concatenate([t.reshape(8, 16, -1, 4), np.zeros((8, 16, 1, 4), BF)], axis=2)
    return np.ascontiguousarray(np.stack([v[g][:, e[g]] for g in range(8)])).reshape(128, -1)
def tile(rs):
    return np.stack(rs, axis=2).reshape(128, -1).astype(BF)
def pick(q, e):
    c = np.concatenate([q[0].reshape(128, -1, 4), np.zeros((128, 1, 4), np.uint8)], axis=1); s = np.concatenate([q[1], np.ones((16, 1), np.uint8)], axis=1)
    return (np.ascontiguousarray(c[:, e].reshape(128, -1)), np.ascontiguousarray(s[:, e]))
def join(*qs):
    return (np.concatenate([q[0] for q in qs], axis=1), np.concatenate([q[1] for q in qs], axis=1))
def put(q, e, v):
    c, s = q[0].reshape(128, -1, 4).copy(), q[1].copy(); c[:, e] = v[0].reshape(128, -1, 4); s[:, e] = v[1]
    return (c.reshape(128, -1), s)
def pk(c, s):
    return (np.ascontiguousarray(c), mx_ref.live(s))
def emit(q):
    return q[0], q[1]
def packed(v, rng):
    q = [mx_ref.quantize(np.ascontiguousarray(v[r])) for r in range(N)]
    return np.stack([a for a, b in q]), np.stack([mx_ref.plane(b, rng) for a, b in q])
def values_of_codes():
    e, c = np.zeros((128, 128, 4), np.float32), np.zeros((128, 2, 4), np.uint8)
    e[np.arange(128), np.arange(128), 0] = 1
    c[:127, :, 0] = np.arange(256).reshape(2, 128).T[:127]
    return mx_ref.matmul(mx_ref.quantize(e.reshape(128, 512).astype(BF)), (c.reshape(128, 8), np.full((16, 2), 127, np.uint8))).T.reshape(-1).astype(np.float64)
CODE_VALUE, SCALE_VALUE = values_of_codes(), 2.0 ** (np.arange(256) - 127.0)
def decode(q):
    return (CODE_VALUE[q[0]].reshape(16, 8, -1, 4) * SCALE_VALUE[q[1]][:, None, :, None] + 0.0).reshape(128, -1).astype(np.float32)
def f(rng, *shape):
    return mx_ref.flush((rng.standard_normal(shape, dtype=np.float32) * np.exp2(rng.integers(-2, 3, shape[:-1] + (1,)))).astype(BF))
def wide(rng, *shape, cols=0):
    v = rng.standard_normal(shape, dtype=np.float32) * np.exp2(rng.integers(-12, 13, shape)).astype(np.float32)
    if cols: v *= np.repeat(np.exp2(rng.integers(-cols, cols + 1, shape[:-2] + (1, shape[-1] // 4))) * (rng.random(shape[:-2] + (1, shape[-1] // 4)) > 0.0625), 4, axis=-1).astype(np.float32)
    return mx_ref.flush(v.astype(BF))
C, K, R = 320, 80, 3
def rings(o):
    e = np.zeros((N, 8, C), int)
    np.put_along_axis(e, o, np.roll(o, -1, axis=2), axis=2)
    return np.stack([gtable(e[r]) for r in range(N)])
def orders(rng):
    return np.argsort(rng.random((N, 8, C)), axis=2)
def numbers_of(rng):
    return {"x": np.array(f(rng, N, 128, 4 * C)), "u": np.array(f(rng, N, 128, 512)), "v": np.array(f(rng, N, 128, 512))}
def layers(rng):
    return np.array(f(rng, N, 128, 2048)).reshape(N, 8, 16, 4, 8, 16, 4)
def carry(source, size):
    w = np.zeros((N, 128, 4, 128, 4), np.float32)
    i = np.arange(128)
    for b in range(4): w[:, i - i % 16 + np.array(source)[i % 16], b, i, b] = 32 * np.resize(size, 128)
    return w.astype(BF)
def weights(rng, w):
    c, p = packed(np.ascontiguousarray(w).reshape(N, 128, 2048), rng)
    return {"wc": c, "ws": p}
def signs(rng):
    return np.stack([rng.permutation(8) % 2 * 2.0 - 1.0 for r in range(N)])
def setup_inputs(rng):
    return {**numbers_of(rng), **weights(rng, layers(rng)), "nx": rings(orders(rng))}
def setup_inputs_ties(rng):
    d = numbers_of(rng)
    x = d["x"].astype(np.float32).reshape(N, 8, 16, C, 4)
    e = (rng.integers(N) + np.arange(N)) % N
    w = layers(rng)
    o = orders(rng)
    for i in range(N):
        r = e[i]
        k = np.stack([rng.permutation(C) % 3 - 1 for g in range(8)])
        if i < 2: k[:] = i
        x[r][:, :8] = np.abs(x[r][:, :8, :1]) * k[:, None, :, None]
        if i >= 3 and i % 2 == 1: w[r][:, :, :, :, :8] = 0
        g = rng.permutation(8)
        o[r, g[0]] = np.arange(C)
        o[r, g[1]] = np.arange(C)[::-1]
    u = d["u"].astype(np.float32).reshape(N, 8, 16, 8, 16, 4)
    k = np.abs(u)
    u[:, :, :, :, 0] = 0
    for g in range(8): u[:, g, :8, g, 0] = k[:, g, :8, g, 0]
    return {"x": x.reshape(N, 128, 4 * C).astype(BF), "u": u.reshape(N, 128, 512).astype(BF), "v": d["v"], **weights(rng, w), "nx": rings(o)}
def setup_inputs_near(rng):
    d = numbers_of(rng)
    x = d["x"].astype(np.float32).reshape(N, 8, 16, C, 4)
    x[:, :, :2] = 0
    u = d["u"].reshape(N, 128, 128, 4)
    u[:, :, ::16] = 0
    e = rng.permutation(8)
    for g in range(8):
        if e[g] < 4:
            s, size, k = rng.integers(-2, 3, (N, 2, C)), 2.0 ** -30, 2.0 ** -30
        else:
            s, size, k = rng.integers(0, 16, (N, 2, C)), 2.0 ** -23, 1.0
            x[:, g, 0, :, 0] = rng.choice([-1.0, 1.0], (N, C))
            x[:, g, 1, :, 0] = e[g] % 2 * 2.0 - 1.0
        x[:, g, 8:10] = ((np.abs(s)[..., None] >> np.arange(4)) & 1) * np.sign(s)[..., None] * np.exp2(np.arange(4.0)) * size
        x[:, g, 10:] = rng.integers(4, 8, (N, 6, C, 4)) * 2 * size
        u[:, 16 * g, 16 * g, 0] = k
        u[:, 16 * g + 8, 16 * g] = k
    times = np.resize(np.array([1.0, 1.0] + [0.75] * 6 + [1.0, 1.0] + [0.75] * 6), (8, 16))
    times[e < 4, 8:10] = 2.0 ** -7
    w = carry([1, 1, 2, 3, 4, 5, 6, 7, 9, 8, 10, 11, 12, 13, 14, 15], times)
    return {"x": x.reshape(N, 128, 4 * C).astype(BF), "u": u.reshape(N, 128, 512), "v": d["v"], **weights(rng, w), "nx": rings(orders(rng))}
def setup_inputs_huge(rng):
    d = numbers_of(rng)
    x = 2.0 ** 30 * (0.8 + 0.2 * rng.random((N, 8, 16, C, 4)))
    for r in range(N): x[r, :, :8] *= (rng.permutation(C) % 2 * 2.0 - 1.0)[:, None]
    u = d["u"].reshape(N, 8, 16, 8, 16, 4)
    u[:, :, :, :, 0] = 0
    a = 2.0 ** 30 * (0.8 + 0.2 * rng.random((N, 8, 8, 8, 4))) * signs(rng)[:, None, None, :, None]
    u[:, :, :8, :, 0] = a.astype(np.float32).astype(BF)
    w = carry([8, 9, 10, 11, 12, 13, 14, 15, 0, 1, 2, 3, 4, 5, 6, 7], [0.875] * 16)
    o = np.zeros((N, 8, C), int) + rng.permutation(C)
    return {"x": x.astype(np.float32).reshape(N, 128, 4 * C).astype(BF), "u": u.reshape(N, 128, 512), "v": d["v"], **weights(rng, w), "nx": rings(o)}
def setup_inputs_slots(rng):
    d = numbers_of(rng)
    n = [0, 1, C // 2, K + 1, K, K - 1, K, K + 1]
    e = rng.permutation(8)
    o = orders(rng)
    x = d["x"].astype(np.float32).reshape(N, 8, 16, C, 4)
    for r in range(N):
        for g in range(8):
            turns = np.sort(rng.permutation(C)[:2 * n[(e[g] + r) % 8]])
            s = (np.searchsorted(turns, np.arange(C), side="right") + rng.integers(2)) % 2
            x[r, g, 0][o[r, g], 0] = 2.0 * s - 1.0
    u = d["u"].reshape(N, 128, 128, 4)
    u[:, :, ::16] = 0
    for h in range(0, 128, 16): u[:, h, h, 0] = 1
    return {"x": x.reshape(N, 128, 4 * C).astype(BF), "u": u.reshape(N, 128, 512), "v": d["v"], **weights(rng, layers(rng)), "nx": rings(o)}
def setup_inputs_spread(rng):
    d = setup_inputs(rng)
    d["x"] = wide(rng, N, 128, 4 * C, cols=6)
    return d
def check_inputs(d):
    b = []
    for k in ("x", "u", "v"):
        a = np.abs(d[k].astype(np.float32))
        if not (np.isfinite(a).all() and ((a == 0) | (a >= 2.0 ** -30) & (a <= 2.0 ** 30)).all()): b.append("a value of " + k)
    if ((d["wc"] & 0x7F) == 0x7F).any(): b.append("a code of wc that is no number")
    z = np.zeros((128, 4, 4), np.float32)
    z[:, 1] = 2.0 ** -30
    z[:, 2] = 2.0 ** 30
    c, s = emit(mx_ref.quantize(z.reshape(128, 16).astype(BF)))
    for r in range(N):
        p = mx_ref.live(d["ws"][r])
        if not ((p == s[0, 0]) | (p >= s[0, 1]) & (p <= s[0, 2])).all(): b.append("a scale of ws")
        e = gentries(d["nx"][r])
        good = bool(((e >= 0) & (e < C)).all())
        j = np.zeros(8, int)
        for i in range(C):
            if good:
                j = e[np.arange(8), j]
                good = bool(((j == 0) == (i == C - 1)).all())
        if not good: b.append("a ring of nx")
    return b
def reference(x, u, v, wc, ws, nx):
    qu = [mx_ref.quantize(u[r]) for r in range(N)]
    lay = [pk(wc[r], ws[r]) for r in range(N)]
    after = [gentries(nx[r]) for r in range(N)]
    before = [np.argsort(after[r], axis=1) for r in range(N)]
    now = [x[r] for r in range(N)]
    for t in range(R):
        forward, parts, sent, count = [], [], [], []
        for r in range(N):
            q = mx_ref.quantize(now[r])
            a = mx_ref.matmul(qu[r], q)[::16] > 0
            p = decode(q).astype(BF)
            e, n = np.full((8, 2 * K), -1), np.zeros(8, int)
            for g in range(8):
                j = np.flatnonzero(a[g] & ~a[g][after[r][g]])[:K]
                n[g] = len(j)
                e[g, 0:2 * len(j):2] = j
                e[g, 1:2 * len(j):2] = after[r][g][j]
            forward.append(a)
            parts.append(p)
            sent.append(mx_ref.quantize(gcols(p, e)))
            count.append(n)
        made, lists = [], []
        for r in range(N):
            z, n = sent[r - 1], count[r - 1]
            h = tile([mx_ref.matmul(pick(lay[r], np.arange(128 * b, 128 * b + 128)), z) * np.float32(0.03125) for b in range(4)])
            p = mx_ref.matmul(qu[r], mx_ref.quantize(h))[::16]
            swap = (p[:, 1::2] > p[:, 0::2]).astype(int)
            e = np.where(forward[r], before[r], after[r])
            for g in range(8):
                a, o = forward[r][g], after[r][g]
                j = np.flatnonzero(~a & a[o])
                e[g, j] = j
                e[g, o[j]] = o[j]
                j = j[:n[g]]
                k = np.arange(len(j))
                e[g, j] = C + 2 * k + swap[g, k]
                e[g, o[j]] = C + 2 * k + 1 - swap[g, k]
            made.append(gcols(np.concatenate([parts[r], h], axis=1), e))
            lists.append(e)
        now = made
    y, ot = np.zeros((N, 128, C), np.float32), np.zeros((N, 8, C), np.float32)
    oc, osc = np.zeros((N, 128, 4 * C), np.uint8), np.zeros((N, 16, C), np.uint8)
    for r in range(N):
        q = mx_ref.quantize(now[r])
        y[r] = mx_ref.matmul(mx_ref.quantize(v[r]), q)
        ot[r] = lists[r]
        oc[r], osc[r] = emit(q)
    return {"y": y, "ot": ot, "oc": oc, "osc": osc}

@@ -1,0 +1,449 @@
+import numpy as np
+from concourse.mybir import dt, AluOpType, AxisListType, ActivationFunctionType
+
+ALU = AluOpType
+ACT = ActivationFunctionType
+C, K, R, N = 320, 80, 3, 4
+CUT = (0, 192, C)
+P2 = 2 * K
+TW = C + P2
+AW = C + 16
+OFF, BIG = 1024.0, 4096.0
+HALF = "float16"
+
+
+def _layout(sizes, align):
+    at, pos = {}, 0
+    for name, n in sizes:
+        at[name] = pos
+        pos += -(-n // align) * align
+    return at, pos
+
+
+LB, LBW = _layout([("F", C), ("F2", C), ("M", C), ("C", C), ("B", C), ("CB", C), ("BR", C), ("BR2", C), ("K", C),
+                   ("JS", 3 * C), ("JV", 2 * C), ("WD", 176)], 16)
+LH, LHW = _layout([("NXA", K), ("NXR", K), ("KR", C), ("FR", C), ("V", C), ("VR", C)], 16)
+LF, LFW = _layout([("HB", C), ("ACC", 8), ("PS", K), ("KW", 20), ("FW", 20), ("T1", 20), ("O", 20), ("Z", 20), ("T2", 20),
+                   ("T3", 20), ("HU", 20), ("T5", 20), ("T6", 20), ("KK", 40), ("DT", 40), ("O2", 40), ("U", 40), ("MM", 40),
+                   ("RR", 40), ("NP", 2)], 8)
+
+X4 = "float8_e4m3fn_x4"
+SCRATCH = {
+    "iotaf": ("sbuf", [128, TW], "float32"), "mi": ("sbuf", [128, C], "int32"), "mj": ("sbuf", [128, C], "int32"),
+    "m0": ("sbuf", [128, C], HALF), "m1": ("sbuf", [128, C], HALF), "dmask": ("sbuf", [128, C], HALF),
+    "pi": ("sbuf", [128, 20], "int32"), "pj": ("sbuf", [128, 20], "int32"), "j0": ("sbuf", [128, 20], "int32"),
+    "jw": ("sbuf", [128, 20], "float32"), "offp": ("sbuf", [128, 2], "float32"), "kb": ("sbuf", [128, 8], "float32"),
+    "uli": ("sbuf", [128, 8], "int32"), "ul": ("sbuf", [128, 8], "uint16"),
+    "ones": ("sbuf", [128, 128], "bfloat16"), "eb": ("sbuf", [128, 516], "bfloat16"),
+    "ec": ("sbuf", [128, 512], X4), "es": ("sbuf", [128, 512], "uint8"),
+    "ut": ("sbuf", [128, 512], "bfloat16"), "uc": ("sbuf", [128, 128], X4), "us": ("sbuf", [128, 128], "uint8"),
+    "upc": ("sbuf", [128, 128], X4), "ups": ("sbuf", [128, 128], "uint8"),
+    "vt": ("sbuf", [128, 512], "bfloat16"), "vc": ("sbuf", [128, 128], X4), "vs": ("sbuf", [128, 128], "uint8"),
+    "lwc": ("sbuf", [128, 512], X4), "lws": ("sbuf", [128, 512], "uint8"),
+    "nxi": ("sbuf", [128, 20], "int32"), "nx16": ("sbuf", [128, 20], "uint16"), "nxw": ("sbuf", [128, 20], "float32"),
+    "nxf": ("sbuf", [128, AW], "float32"), "pvf": ("sbuf", [128, C], "float32"), "pvr": ("sbuf", [128, C], "float32"),
+    "pvw": ("sbuf", [128, 20], "float32"), "pv16": ("sbuf", [128, 20], "uint16"), "dpn": ("sbuf", [128, 20], "float32"),
+    "lb": ("sbuf", [128, R * LBW], "bfloat16"), "lf": ("sbuf", [128, R * LFW], "float32"), "lh": ("sbuf", [128, R * LHW], HALF),
+    "yt": ("sbuf", [128, C], "float32"), "ott": ("sbuf", [128, C], "float32"),
+}
+for _t in range(R + 1):
+    SCRATCH["x%d" % _t] = ("sbuf", [128, 4 * C], "bfloat16")
+    SCRATCH["qc%d" % _t] = ("sbuf", [128, C], X4)
+    SCRATCH["qs%d" % _t] = ("sbuf", [128, C], "uint8")
+for _t in range(R):
+    SCRATCH["tp%d" % _t] = ("sbuf", [128, 4 * TW], "bfloat16")
+    SCRATCH["ta%d" % _t] = ("sbuf", [128, 4 * AW], "bfloat16")
+    SCRATCH["lc%d" % _t] = ("sbuf", [128, C], X4)
+    SCRATCH["ls%d" % _t] = ("sbuf", [128, C], "uint8")
+    SCRATCH["at%d" % _t] = ("sbuf", [128, 4 * P2], "bfloat16")
+    SCRATCH["ac%d" % _t] = ("sbuf", [128, P2], X4)
+    SCRATCH["as%d" % _t] = ("sbuf", [128, P2], "uint8")
+    SCRATCH["ht%d" % _t] = ("sbuf", [128, 4 * P2], "bfloat16")
+    SCRATCH["hc%d" % _t] = ("sbuf", [128, P2], X4)
+    SCRATCH["hs%d" % _t] = ("sbuf", [128, P2], "uint8")
+    SCRATCH["sl%d" % _t] = ("sbuf", [128, 12], "uint16")
+    SCRATCH["ll%d" % _t] = ("sbuf", [128, 12], "uint16")
+    SCRATCH["hk%d" % _t] = ("sbuf", [128, 40], "uint16")
+    SCRATCH["h%d" % _t] = ("sbuf", [128, 20], "uint16")
+for _b in range(8):
+    SCRATCH["ps%d" % _b] = ("psum", [128, 512], "float32")
+
+SEMAPHORES = (["cv", "cs", "ct", "cg", "loc"] + ["d%d" % i for i in range(20)]
+              + [s + "%d" % t for t in range(R) for s in ("ra", "rb", "rs", "rl")])
+
+
+def _cols(a, b, step=1):
+    m = 0
+    for c in range(a, b, step):
+        m |= 1 << c
+    return m
+
+
+def _machine(g, T):
+    queues = {"v": g.vector, "s": g.scalar, "t": g.tensor, "g": g, "y": g.sync}
+    total, clock, hist, fresh = {}, {}, {}, [0]
+    known = dict((q, {}) for q in queues)
+
+    def wait(q, sem, val):
+        if known[q].get(sem, 0) >= val:
+            return
+        queues[q].wait_ge(T.sem[sem], val)
+        for s, n in clock.get((sem, val), {}).items():
+            known[q][s] = max(known[q].get(s, 0), n)
+        known[q][sem] = max(known[q].get(sem, 0), val)
+
+    def order(q, writes, reads):
+        need = {}
+        for acc, wr in [(a, True) for a in writes] + [(a, False) for a in reads]:
+            for mask, oq, sem, val, owr in hist.get(acc[1], []):
+                if not mask & acc[2]:
+                    continue
+                if wr and not owr and oq == q:
+                    continue
+                if not wr and not owr and (oq == q or not acc[1].startswith("ps")):
+                    continue
+                need[sem] = max(need.get(sem, 0), val)
+        need = [(s, n) for s, n in need.items() if known[q].get(s, 0) < n]
+        for s, n in need:
+            if not any(clock.get(o, {}).get(s, 0) >= n for o in need if o != (s, n)):
+                wait(q, s, n)
+
+    def note(q, sem, val, writes, reads):
+        for a in writes:
+            hist.setdefault(a[1], []).append((a[2], q, sem, val, True))
+        for a in reads:
+            hist.setdefault(a[1], []).append((a[2], q, sem, val, False))
+
+    def op(q, call, writes, reads):
+        order(q, writes, reads)
+        sem = "c" + q
+        val = total[sem] = total.get(sem, 0) + 1
+        call(queues[q]).then_inc(T.sem[sem], 1)
+        clock[(sem, val)] = dict(known[q])
+        note(q, sem, val, writes, reads)
+
+    def dma(q, out, in_, writes, reads):
+        order(q, writes, reads)
+        sem = "d%d" % fresh[0]
+        fresh[0] += 1
+        total[sem] = 16
+        queues[q].dma_start(out, in_).then_inc(T.sem[sem], 16)
+        clock[(sem, 16)] = dict(known[q])
+        note("d", sem, 16, writes, reads)
+
+    def send(out, in_, rsem, where, reads, engines):
+        order("g", [], reads)
+        total["loc"] = total.get("loc", 0) + engines
+        g.remote_dma(out, in_, T.sem[rsem], T.sem.loc, where[0], where[1], where[2])
+
+    def lands(writes, rsem, engines):
+        total[rsem] = engines
+        note("net", rsem, engines, writes, [])
+
+    def close():
+        for sem in sorted(total):
+            wait("g", sem, total[sem])
+
+    return op, dma, send, lands, close
+
+
+def rank_program(g, core, T, topo):
+    rank = T.rank_of(core)
+    if rank is None:
+        return
+    op, dma, send, lands, close = _machine(g, T)
+    dst, src = T.cores[(rank + 1) % N], T.cores[rank - 1]
+    rid, pid = topo.addr(dst)[:2]
+    where = (pid, rid, topo.mask(core, dst))
+    n_out, n_in = len(topo.engines(core, dst)), len(topo.engines(src, core))
+
+    def A(name, a, b, step=1):
+        return (T[name][:, a:b:step] if step > 1 else T[name][:, a:b], name, _cols(a, b, step))
+
+    def lb(t, key, n, a=0, step=1):
+        o = t * LBW + LB[key]
+        return A("lb", o + a, o + n, step)
+
+    def lf(t, key, n, a=0, step=1):
+        o = t * LFW + LF[key]
+        return A("lf", o + a, o + n, step)
+
+    def lh(t, key, n, a=0, step=1):
+        o = t * LHW + LH[key]
+        return A("lh", o + a, o + n, step)
+
+    def U8(acc):
+        return acc[0].bitcast(dt.uint8)
+
+    def E(b):
+        return A("ec", 128 * b, 128 * b + 128), A("es", 128 * b, 128 * b + 128)
+
+    def W(b):
+        return A("lwc", 128 * b, 128 * b + 128), A("lws", 128 * b, 128 * b + 128)
+
+    def fill(out, value):
+        op("v", lambda q: q.memset(out[0], value), [out], [])
+
+    def copy(out, in_):
+        op("v", lambda q: q.tensor_copy(out[0], in_[0]), [out], [in_])
+
+    def pick(q, out, win, off):
+        if q == "v":
+            op("v", lambda e: e.tensor_copy(out[0], win[0].indirect(off[0])), [out], [win, off])
+        else:
+            op("s", lambda e: e.activation(out[0], win[0].indirect(off[0]), ACT.Copy), [out], [win, off])
+
+    def scalar1(out, in0, s1, op0, s2=None, op1=None):
+        reads = [in0] + ([s1] if isinstance(s1, tuple) else [])
+        a1 = s1[0] if isinstance(s1, tuple) else s1
+        if op1 is None:
+            op("v", lambda q: q.tensor_scalar(out[0], in0[0], a1, None, op0), [out], reads)
+        else:
+            op("v", lambda q: q.tensor_scalar(out[0], in0[0], a1, s2, op0, op1), [out], reads)
+
+    def two(out, in0, in1, o):
+        op("v", lambda q: q.tensor_tensor(out[0], in0[0], in1[0], o), [out], [in0, in1])
+
+    def two_at(out, win, off, in1, o):
+        op("v", lambda q: q.tensor_tensor(out[0], win[0].indirect(off[0]), in1[0], o), [out], [win, off, in1])
+
+    def scan(out, d0, d1, op0, op1):
+        op("v", lambda q: q.tensor_tensor_scan(out[0], d0[0], d1[0], 0.0, op0, op1), [out], [d0, d1])
+
+    def diagonal(raw, rows, n):
+        scan(raw, A("dmask", 0, n), rows, ALU.add, ALU.max)
+
+    def prefix(out, flags):
+        scan(out, flags, flags, ALU.add, ALU.max)
+
+    def quant(c, s, tile):
+        op("v", lambda q: q.quantize_mx(c[0], s[0], tile[0]), [c, s], [tile])
+
+    def mm(bank, w, xc, xs, n):
+        out = A("ps%d" % bank, 0, n)
+        op("t", lambda q: q.matmul_mx(out[0], w[0][0], w[1][0], xc[0], xs[0], True, True), [out], [w[0], w[1], xc, xs])
+
+    def act(out, in_, scale=None):
+        if scale is None:
+            op("s", lambda q: q.activation(out[0], in_[0], ACT.Copy), [out], [in_])
+        else:
+            op("s", lambda q: q.activation(out[0], in_[0], ACT.Copy, scale=scale), [out], [in_])
+
+    def load(q, name, a, b, ap):
+        w = A(name, a, b)
+        dma(q, w[0], ap, [w], [])
+
+    def iota(out, pattern, base, ch):
+        op("g", lambda q: q.iota(out[0], pattern, base, ch), [out], [])
+
+    def state_codes(t, h):
+        a, b = CUT[h], CUT[h + 1]
+        quant(A("qc%d" % t, a, b), A("qs%d" % t, a, b), A("x%d" % t, 4 * a, 4 * b))
+
+    def send_codes(t, h):
+        i = A("qc%d" % t, CUT[h], CUT[h + 1])
+        send(U8(A("lc%d" % t, CUT[h], CUT[h + 1])), U8(i), ("ra%d", "rb%d")[h] % t, where, [i], n_out)
+
+    def send_scales(t):
+        i = A("qs%d" % t, 0, C)
+        send(A("ls%d" % t, 0, C)[0], i[0], "rs%d" % t, where, [i], n_out)
+
+    load("y", "x0", 0, 4 * CUT[1], T.x[:, 0:4 * CUT[1]])
+    load("s", "ut", 0, 512, T.u[:, :])
+    load("y", "x0", 4 * CUT[1], 4 * C, T.x[:, 4 * CUT[1]:4 * C])
+    load("s", "nxi", 0, 20, T.nx[:, :])
+    w = A("lwc", 0, 512)
+    dma("y", U8(w), T.wc[:, :], [w], [])
+    load("s", "lws", 0, 512, T.ws[:, :])
+    load("y", "vt", 0, 512, T.v[:, :])
+    for t in range(R):
+        lands([A("lc%d" % t, 0, CUT[1])], "ra%d" % t, n_in)
+        lands([A("lc%d" % t, CUT[1], C)], "rb%d" % t, n_in)
+        lands([A("ls%d" % t, 0, C)], "rs%d" % t, n_in)
+        lands([A("ll%d" % t, 0, 12)], "rl%d" % t, n_in)
+
+    fill(A("ones", 0, 128), 1.0)
+    fill(A("eb", 0, 516), 0.0)
+    iota(A("uli", 0, 8), [[16, 8]], 0, 0)
+    e, o = A("eb", 3, 515, 4), A("ones", 0, 128)
+    op("g", lambda q: q.affine_select(e[0], o[0], [[-1, 128]], ALU.is_equal, 0.0, 0, 1), [e], [o])
+    iota(A("mi", 0, C), [[1, C]], 128, -1)
+    iota(A("pi", 0, 20), [[0, 20]], 0, 1)
+    iota(A("j0", 0, 20), [[16, 20]], 0, 0)
+    fi = A("iotaf", 0, TW)
+    op("g", lambda q: q.iota(fi[0], [[1, TW]], 0, 0, allow_small_or_imprecise_dtypes=True), [fi], [])
+    copy(A("ul", 0, 8), A("uli", 0, 8))
+    for b in range(4):
+        quant(E(b)[0], E(b)[1], A("eb", 3 - b, 515 - b))
+    scalar1(A("mj", 0, C), A("mi", 0, C), 15, ALU.bitwise_and)
+    scalar1(A("m0", 0, C), A("mj", 0, C), 0.0, ALU.is_equal, -BIG, ALU.mult)
+    scalar1(A("m1", 0, C), A("mj", 0, C), 1.0, ALU.is_equal, OFF, ALU.mult)
+    scalar1(A("pj", 0, 20), A("pi", 0, 20), 15, ALU.bitwise_and)
+    fill(A("nxf", C, AW), float(C))
+    two(A("jw", 0, 20), A("j0", 0, 20), A("pj", 0, 20), ALU.add)
+    scalar1(A("offp", 0, 2), A("pj", 0, 2), 14.5, ALU.is_lt, OFF, ALU.mult)
+    scalar1(A("kb", 0, 5), A("jw", 0, 5), 0.5, ALU.add)
+    state_codes(0, 0)
+    send_codes(0, 0)
+    quant(A("uc", 0, 128), A("us", 0, 128), A("ut", 0, 512))
+    up, ic_, ul = (A("upc", 0, 128), A("ups", 0, 128)), A("uc", 0, 128), A("ul", 0, 8)
+    op("v", lambda q: q.tensor_copy(up[0][0].bitcast(dt.uint32), ic_[0].bitcast(dt.uint32).indirect(ul[0])), [up[0]], [ic_, ul])
+    pick("s", up[1], A("us", 0, 128), ul)
+    state_codes(0, 1)
+    copy(A("nx16", 0, 20), A("nxi", 0, 20))
+    pick("s", A("nxf", 0, C), A("iotaf", 0, C), A("nx16", 0, 20))
+    offp = A("offp", 0, 1)
+
+    for t in range(R):
+        n = lambda s: "%s%d" % (s, t)
+        qc, qs = A(n("qc"), 0, C), A(n("qs"), 0, C)
+        F, F2, M, Cn, B = lb(t, "F", C), lb(t, "F2", C), lb(t, "M", C), lb(t, "C", C), lb(t, "B", C)
+        send_scales(t)
+        send_codes(t, 1)
+        for h in range(2):
+            a, z = CUT[h], CUT[h + 1]
+            mm(4 + h, up, A(n("qc"), a, z), A(n("qs"), a, z), z - a)
+        for b in range(4):
+            mm(b, E(b), qc, qs, C)
+        for h in range(2):
+            a, z = CUT[h], CUT[h + 1]
+            scalar1(lb(t, "F", z, a), A("ps%d" % (4 + h), 0, z - a), 0.0, ALU.is_gt)
+            if h == 0:
+                act(lb(t, "F2", z, a), lb(t, "F", z, a))
+            else:
+                scalar1(lb(t, "F2", z, a), A("ps%d" % (4 + h), 0, z - a), 0.0, ALU.is_gt)
+        two_at(M, F, A("nx16", 0, 20), F2, ALU.is_lt)
+
+        def own(b):
+            act(A(n("tp"), TW * b, TW * b + C), A("ps%d" % b, 0, C))
+
+        own(0)
+        own(1)
+        prefix(Cn, M)
+        sl = A(n("sl"), 0, 12)
+        for m in range(3):
+            j, acc = lb(t, "JS", C * m + C, C * m), lf(t, "ACC", m + 1, m)
+            kb = A("kb", m, m + 1)
+            op("s", lambda q, j=j, acc=acc, kb=kb: q.activation(j[0], Cn[0], ACT.Sign, bias=kb[0], scale=-1.0, accum_out=acc[0]),
+               [j, acc], [Cn, kb])
+        for m in (3, 4):
+            scalar1(lb(t, "JV", C * (m - 3) + C, C * (m - 3)), Cn, A("jw", m, m + 1), ALU.is_le)
+        for m in (3, 4):
+            j, acc = lb(t, "JV", C * (m - 3) + C, C * (m - 3)), lf(t, "ACC", m + 1, m)
+            op("v", lambda q, j=j, acc=acc: q.tensor_reduce(acc[0], j[0], AxisListType.X, ALU.add), [acc], [j])
+        copy(A(n("sl"), 3, 5), lf(t, "ACC", 5, 3))
+        if t == 0:
+            two(A("dmask", 0, C), A("m0", 0, C), A("m1", 0, C), ALU.add)
+        scalar1(A(n("sl"), 0, 3), lf(t, "ACC", 3), 0.5, ALU.mult, C / 2.0, ALU.add)
+        pick("v", lh(t, "NXA", K), A("nxf", 0, AW), A(n("sl"), 0, 5))
+        scalar1(A(n("sl"), 10, 12), lb(t, "C", C, C - 2), float(K), ALU.min)
+        diagonal(lh(t, "NXR", K), lh(t, "NXA", K), K)
+        scalar1(A(n("sl"), 5, 10), lh(t, "NXR", K, 15, 16), offp, ALU.subtract)
+        send(A(n("ll"), 0, 12)[0], sl[0], n("rl"), where, [sl], n_out)
+
+        own(2)
+        own(3)
+        if t == 0:
+            for r in range(R):
+                for b in range(4):
+                    fill(A("ta%d" % r, AW * b + C, AW * b + AW), 0.0)
+                fill(lb(r, "WD", 176), 0.0)
+                fill(lf(r, "O2", 40), 0.0)
+            pf, io, nx16 = A("pvf", 0, C), A("iotaf", 0, C), A("nx16", 0, 20)
+            op("v", lambda q: q.tensor_copy(pf[0].indirect(nx16[0]), io[0]), [pf], [io, nx16])
+            copy(A("nxw", 0, 20), A("nxi", 0, 20))
+        two_at(B, F, A("nx16", 0, 20), F2, ALU.is_gt)
+        if t == 0:
+            diagonal(A("pvr", 0, C), pf, C)
+        prefix(lb(t, "CB", C), B)
+        if t == 0:
+            scalar1(A("pv16", 0, 20), A("pvr", 15, C, 16), offp, ALU.subtract)
+            scalar1(A("pvw", 0, 20), A("pvr", 15, C, 16), offp, ALU.subtract)
+        diagonal(lh(t, "FR", C), F, C)
+        two(lb(t, "BR", C), B, lb(t, "CB", C), ALU.mult)
+        act(lb(t, "BR2", C), lb(t, "BR", C))
+        if t == 0:
+            two(A("dpn", 0, 20), A("pvw", 0, 20), A("nxw", 0, 20), ALU.subtract)
+        scalar1(lf(t, "FW", 20), lh(t, "FR", C, 15, 16), offp, ALU.subtract)
+        two(lf(t, "T1", 20), lf(t, "FW", 20), A("dpn", 0, 20), ALU.mult)
+        two(lf(t, "O", 20), lf(t, "T1", 20), A("nxw", 0, 20), ALU.add)
+        scalar1(lf(t, "T5", 20), lf(t, "FW", 20), float(K), ALU.mult)
+        two(lf(t, "T2", 20), A("jw", 0, 20), lf(t, "O", 20), ALU.subtract)
+        two_at(lb(t, "K", C), lb(t, "BR", C), A("pv16", 0, 20), lb(t, "BR2", C), ALU.add)
+        diagonal(lh(t, "KR", C), lb(t, "K", C), C)
+        KW = lf(t, "KW", 20)
+        scalar1(KW, lh(t, "KR", C, 15, 16), offp, ALU.subtract)
+        scalar1(lf(t, "Z", 20), KW, 0.5, ALU.is_gt)
+        scalar1(lf(t, "T6", 20), KW, 0.5, ALU.is_lt, 1000.0, ALU.mult)
+        scalar1(lf(t, "HU", 20), KW, 2.0, ALU.mult, C - 2.0, ALU.add)
+        two(lf(t, "T3", 20), lf(t, "T2", 20), lf(t, "Z", 20), ALU.mult)
+
+        for h in range(2):
+            a, z = CUT[h], CUT[h + 1]
+            for b in range(4):
+                bank = b if h else 4 + b
+                mm(bank, E(b), A(n("lc"), a, z), A(n("ls"), a, z), z - a)
+                act(A(n("ta"), AW * b + a, AW * b + z), A("ps%d" % bank, 0, z - a))
+        for b in range(4):
+            pick("vvss"[b], A(n("at"), b, 4 * P2, 4), A(n("ta"), AW * b, AW * b + AW), A(n("ll"), 0, 10))
+        ac, as_ = A(n("ac"), 0, P2), A(n("as"), 0, P2)
+        quant(ac, as_, A(n("at"), 0, 4 * P2))
+        for b in range(4):
+            mm(b, W(b), ac, as_, P2)
+        copy(lf(t, "NP", 2), A(n("ll"), 10, 12))
+        two(lf(t, "KK", 20), lf(t, "T6", 20), KW, ALU.add)
+        two(lf(t, "KK", 40, 20), lf(t, "T6", 20), KW, ALU.add)
+        two(lf(t, "O2", 20), lf(t, "O", 20), lf(t, "T3", 20), ALU.add)
+        scalar1(lf(t, "U", 40), lf(t, "KK", 40), lf(t, "NP", 2, 1), ALU.is_le)
+        two(lf(t, "DT", 40, 20), lf(t, "T5", 20), KW, ALU.add)
+        two(lf(t, "DT", 20), lf(t, "HU", 20), lf(t, "O2", 20), ALU.subtract)
+        two(lf(t, "MM", 40), lf(t, "U", 40), lf(t, "DT", 40), ALU.mult)
+        two(lf(t, "RR", 40), lf(t, "MM", 40), lf(t, "O2", 40), ALU.add)
+        copy(A(n("hk"), 0, 40), lf(t, "RR", 40))
+        for b in range(4):
+            out, z = A(n("ht"), b, 4 * P2, 4), A("ps%d" % b, 0, P2)
+            if b < 2:
+                act(out, z, 0.03125)
+            else:
+                scalar1(out, z, 0.03125, ALU.mult)
+        hc, hs = A(n("hc"), 0, P2), A(n("hs"), 0, P2)
+        quant(hc, hs, A(n("ht"), 0, 4 * P2))
+        mm(6, up, hc, hs, P2)
+        hb = lf(t, "HB", C)
+        pick("s", hb, A("iotaf", 0, TW), A(n("hk"), 0, 20))
+        for b in range(4):
+            for i in range(2):
+                out, z = A(n("tp"), TW * b + C + i, TW * b + TW, 2), A("ps%d" % b, K * i, K * i + K)
+                if b < 2:
+                    act(out, z, 0.03125)
+                else:
+                    scalar1(out, z, 0.03125, ALU.mult)
+        if t == 1:
+            quant(A("vc", 0, 128), A("vs", 0, 128), A("vt", 0, 512))
+        act(lf(t, "PS", K), A("ps6", 0, K))
+        two(lb(t, "WD", K + 1, 1), lf(t, "PS", K), A("ps6", K, P2), ALU.is_lt)
+        two(lb(t, "WD", P2 + 1, K + 1), lf(t, "PS", K), A("ps6", K, P2), ALU.is_ge)
+        two_at(lh(t, "V", C), lb(t, "WD", 176), A(n("hk"), 20, 40), hb, ALU.add)
+        diagonal(lh(t, "VR", C), lh(t, "V", C), C)
+        scalar1(A(n("h"), 0, 20), lh(t, "VR", C, 15, 16), offp, ALU.subtract)
+        for h in range(2):
+            a, z = CUT[h], CUT[h + 1]
+            for b in range(4):
+                pick("vvss"[b], A("x%d" % (t + 1), 4 * a + b, 4 * z, 4), A(n("tp"), TW * b, TW * b + TW),
+                     A(n("h"), a // 16, z // 16))
+            state_codes(t + 1, h)
+            if h == 0 and t + 1 < R:
+                send_codes(t + 1, 0)
+
+    for h in range(2):
+        a, z = CUT[h], CUT[h + 1]
+        mm(4 + h, (A("vc", 0, 128), A("vs", 0, 128)), A("qc3", a, z), A("qs3", a, z), z - a)
+    dma("y", T.oc[:, :], U8(A("qc3", 0, C)), [], [A("qc3", 0, C)])
+    for k in range(4):
+        dma("y", T.osc[4 * k:4 * k + 4, :], T.qs3[32 * k:32 * k + 4, 0:C], [], [A("qs3", 0, C)])
+    act(A("yt", 0, CUT[1]), A("ps4", 0, CUT[1]))
+    copy(A("yt", CUT[1], C), A("ps5", 0, C - CUT[1]))
+    dma("s", T.y[:, :], A("yt", 0, C)[0], [], [A("yt", 0, C)])
+    copy(A("ott", 0, C), lh(R - 1, "V", C))
+    dma("y", T.ot[:, :], T.ott[0:128:16, 0:C], [], [A("ott", 0, C)])
+    close()

@@ -20,17 +20,15 @@ def _layout(sizes, align):
     return at, pos
 
 
-LB, LBW = _layout([("F", C), ("F2", C), ("M", C), ("C", C), ("B", C), ("CB", C), ("BR", C), ("BR2", C), ("K", C),
-                   ("JS", 3 * C), ("JV", 2 * C), ("WD", 176)], 16)
-LH, LHW = _layout([("NXA", K), ("NXR", K), ("KR", C), ("FR", C), ("V", C), ("VR", C)], 16)
-LF, LFW = _layout([("HB", C), ("ACC", 8), ("PS", K), ("KW", 20), ("FW", 20), ("T1", 20), ("O", 20), ("Z", 20), ("T2", 20),
-                   ("T3", 20), ("HU", 20), ("T5", 20), ("T6", 20), ("KK", 40), ("DT", 40), ("O2", 40), ("U", 40), ("MM", 40),
-                   ("RR", 40), ("NP", 2)], 8)
+LB, LBW = _layout([("F", C), ("F2", C), ("M", C), ("C", C), ("B", C), ("CB", C), ("CBP", C), ("I", C), ("JS", 3 * C)], 16)
+LH, LHW = _layout([("NXA", K), ("NXR", K), ("RAW", 5 * C), ("V", C), ("VR", C)], 16)
+LF, LFW = _layout([("HB", C), ("ACC", 8), ("PS", K), ("W5", 100), ("PR", 40), ("KK", 40), ("X60", 60), ("Y", 20), ("Y2", 20),
+                   ("Z", 20), ("ZC", 20), ("DT", 40), ("U", 40), ("MM", 40), ("RR", 40), ("NP", 2)], 8)
 
 X4 = "float8_e4m3fn_x4"
 SCRATCH = {
-    "iotaf": ("sbuf", [128, TW], "float32"), "mi": ("sbuf", [128, C], "int32"), "mj": ("sbuf", [128, C], "int32"),
-    "m0": ("sbuf", [128, C], HALF), "m1": ("sbuf", [128, C], HALF), "dmask": ("sbuf", [128, C], HALF),
+    "iotaf": ("sbuf", [128, TW], "float32"), "mi": ("sbuf", [128, 16], "int32"), "mj": ("sbuf", [128, 16], "int32"),
+    "m0": ("sbuf", [128, 16], HALF), "m1": ("sbuf", [128, 16], HALF), "dmask": ("sbuf", [128, C], HALF),
     "pi": ("sbuf", [128, 20], "int32"), "pj": ("sbuf", [128, 20], "int32"), "j0": ("sbuf", [128, 20], "int32"),
     "jw": ("sbuf", [128, 20], "float32"), "offp": ("sbuf", [128, 2], "float32"), "kb": ("sbuf", [128, 8], "float32"),
     "uli": ("sbuf", [128, 8], "int32"), "ul": ("sbuf", [128, 8], "uint16"),
@@ -42,7 +40,10 @@ SCRATCH = {
     "lwc": ("sbuf", [128, 512], X4), "lws": ("sbuf", [128, 512], "uint8"),
     "nxi": ("sbuf", [128, 20], "int32"), "nx16": ("sbuf", [128, 20], "uint16"), "nxw": ("sbuf", [128, 20], "float32"),
     "nxf": ("sbuf", [128, AW], "float32"), "pvf": ("sbuf", [128, C], "float32"), "pvr": ("sbuf", [128, C], "float32"),
-    "pvw": ("sbuf", [128, 20], "float32"), "pv16": ("sbuf", [128, 20], "uint16"), "dpn": ("sbuf", [128, 20], "float32"),
+    "pvw": ("sbuf", [128, 20], "float32"), "pv16": ("sbuf", [128, 20], "uint16"), "cj": ("sbuf", [128, 60], "float32"),
+    "cz": ("sbuf", [128, 20], "float32"),
+    "ta": ("sbuf", [128, 4 * AW], "bfloat16"), "wd": ("sbuf", [128, 176], "bfloat16"),
+    "jv": ("sbuf", [128, 2 * AW], "bfloat16"), "o2": ("sbuf", [128, 40], "float32"),
     "lb": ("sbuf", [128, R * LBW], "bfloat16"), "lf": ("sbuf", [128, R * LFW], "float32"), "lh": ("sbuf", [128, R * LHW], HALF),
     "yt": ("sbuf", [128, C], "float32"), "ott": ("sbuf", [128, C], "float32"),
 }
@@ -52,7 +53,6 @@ for _t in range(R + 1):
     SCRATCH["qs%d" % _t] = ("sbuf", [128, C], "uint8")
 for _t in range(R):
     SCRATCH["tp%d" % _t] = ("sbuf", [128, 4 * TW], "bfloat16")
-    SCRATCH["ta%d" % _t] = ("sbuf", [128, 4 * AW], "bfloat16")
     SCRATCH["lc%d" % _t] = ("sbuf", [128, C], X4)
     SCRATCH["ls%d" % _t] = ("sbuf", [128, C], "uint8")
     SCRATCH["at%d" % _t] = ("sbuf", [128, 4 * P2], "bfloat16")
@@ -213,9 +213,6 @@ def rank_program(g, core, T, topo):
     def diagonal(raw, rows, n):
         scan(raw, A("dmask", 0, n), rows, ALU.add, ALU.max)
 
-    def prefix(out, flags):
-        scan(out, flags, flags, ALU.add, ALU.max)
-
     def quant(c, s, tile):
         op("v", lambda q: q.quantize_mx(c[0], s[0], tile[0]), [c, s], [tile])
 
@@ -236,6 +233,9 @@ def rank_program(g, core, T, topo):
     def iota(out, pattern, base, ch):
         op("g", lambda q: q.iota(out[0], pattern, base, ch), [out], [])
 
+    def iota_f(out, step, n, base):
+        op("g", lambda q: q.iota(out[0], [[step, n]], base, 0, allow_small_or_imprecise_dtypes=True), [out], [])
+
     def state_codes(t, h):
         a, b = CUT[h], CUT[h + 1]
         quant(A("qc%d" % t, a, b), A("qs%d" % t, a, b), A("x%d" % t, 4 * a, 4 * b))
@@ -248,10 +248,10 @@ def rank_program(g, core, T, topo):
         i = A("qs%d" % t, 0, C)
         send(A("ls%d" % t, 0, C)[0], i[0], "rs%d" % t, where, [i], n_out)
 
-    load("y", "x0", 0, 4 * CUT[1], T.x[:, 0:4 * CUT[1]])
+    load("y", "nxi", 0, 20, T.nx[:, :])
     load("s", "ut", 0, 512, T.u[:, :])
+    load("y", "x0", 0, 4 * CUT[1], T.x[:, 0:4 * CUT[1]])
     load("y", "x0", 4 * CUT[1], 4 * C, T.x[:, 4 * CUT[1]:4 * C])
-    load("s", "nxi", 0, 20, T.nx[:, :])
     w = A("lwc", 0, 512)
     dma("y", U8(w), T.wc[:, :], [w], [])
     load("s", "lws", 0, 512, T.ws[:, :])
@@ -265,39 +265,53 @@ def rank_program(g, core, T, topo):
     fill(A("ones", 0, 128), 1.0)
     fill(A("eb", 0, 516), 0.0)
     iota(A("uli", 0, 8), [[16, 8]], 0, 0)
-    e, o = A("eb", 3, 515, 4), A("ones", 0, 128)
-    op("g", lambda q: q.affine_select(e[0], o[0], [[-1, 128]], ALU.is_equal, 0.0, 0, 1), [e], [o])
-    iota(A("mi", 0, C), [[1, C]], 128, -1)
+    iota(A("mi", 0, 16), [[1, 16]], 128, -1)
     iota(A("pi", 0, 20), [[0, 20]], 0, 1)
     iota(A("j0", 0, 20), [[16, 20]], 0, 0)
-    fi = A("iotaf", 0, TW)
-    op("g", lambda q: q.iota(fi[0], [[1, TW]], 0, 0, allow_small_or_imprecise_dtypes=True), [fi], [])
+    e, o = A("eb", 3, 515, 4), A("ones", 0, 128)
+    op("g", lambda q: q.affine_select(e[0], o[0], [[-1, 128]], ALU.is_equal, 0.0, 0, 1), [e], [o])
+    iota_f(A("iotaf", 0, TW), 1, TW, 0)
+    for b in range(2):
+        iota_f(A("jv", AW * b + C, AW * b + C + 8), 0, 8, -C)
     copy(A("ul", 0, 8), A("uli", 0, 8))
+    scalar1(A("mj", 0, 16), A("mi", 0, 16), 15, ALU.bitwise_and)
+    scalar1(A("pj", 0, 20), A("pi", 0, 20), 15, ALU.bitwise_and)
+    scalar1(A("m0", 0, 16), A("mj", 0, 16), 0.0, ALU.is_equal, -BIG, ALU.mult)
+    scalar1(A("m1", 0, 16), A("mj", 0, 16), 1.0, ALU.is_equal, OFF, ALU.mult)
+    two(A("jw", 0, 20), A("j0", 0, 20), A("pj", 0, 20), ALU.add)
+    two(A("dmask", 0, 16), A("m0", 0, 16), A("m1", 0, 16), ALU.add)
+    scalar1(A("offp", 0, 2), A("pj", 0, 2), 14.5, ALU.is_lt, OFF, ALU.mult)
     for b in range(4):
         quant(E(b)[0], E(b)[1], A("eb", 3 - b, 515 - b))
-    scalar1(A("mj", 0, C), A("mi", 0, C), 15, ALU.bitwise_and)
-    scalar1(A("m0", 0, C), A("mj", 0, C), 0.0, ALU.is_equal, -BIG, ALU.mult)
-    scalar1(A("m1", 0, C), A("mj", 0, C), 1.0, ALU.is_equal, OFF, ALU.mult)
-    scalar1(A("pj", 0, 20), A("pi", 0, 20), 15, ALU.bitwise_and)
+        copy(A("dmask", 16 << b, 32 << b), A("dmask", 0, 16 << b))
     fill(A("nxf", C, AW), float(C))
-    two(A("jw", 0, 20), A("j0", 0, 20), A("pj", 0, 20), ALU.add)
-    scalar1(A("offp", 0, 2), A("pj", 0, 2), 14.5, ALU.is_lt, OFF, ALU.mult)
+    copy(A("dmask", 256, C), A("dmask", 0, C - 256))
     scalar1(A("kb", 0, 5), A("jw", 0, 5), 0.5, ALU.add)
-    state_codes(0, 0)
-    send_codes(0, 0)
+    copy(A("nx16", 0, 20), A("nxi", 0, 20))
+    copy(A("nxw", 0, 20), A("nxi", 0, 20))
+    scalar1(A("cz", 0, 20), A("jw", 0, 20), -1.0, ALU.mult, C - 2.0, ALU.add)
     quant(A("uc", 0, 128), A("us", 0, 128), A("ut", 0, 512))
     up, ic_, ul = (A("upc", 0, 128), A("ups", 0, 128)), A("uc", 0, 128), A("ul", 0, 8)
     op("v", lambda q: q.tensor_copy(up[0][0].bitcast(dt.uint32), ic_[0].bitcast(dt.uint32).indirect(ul[0])), [up[0]], [ic_, ul])
     pick("s", up[1], A("us", 0, 128), ul)
+    state_codes(0, 0)
+    send_codes(0, 0)
     state_codes(0, 1)
-    copy(A("nx16", 0, 20), A("nxi", 0, 20))
     pick("s", A("nxf", 0, C), A("iotaf", 0, C), A("nx16", 0, 20))
-    offp = A("offp", 0, 1)
+    offp, nx16, pv16, nxw, jw, pvw = A("offp", 0, 1), A("nx16", 0, 20), A("pv16", 0, 20), A("nxw", 0, 20), A("jw", 0, 20), A("pvw", 0, 20)
 
     for t in range(R):
         n = lambda s: "%s%d" % (s, t)
         qc, qs = A(n("qc"), 0, C), A(n("qs"), 0, C)
         F, F2, M, Cn, B = lb(t, "F", C), lb(t, "F2", C), lb(t, "M", C), lb(t, "C", C), lb(t, "B", C)
+        CB, CBP, I, W5, KK, O2 = lb(t, "CB", C), lb(t, "CBP", C), lb(t, "I", C), lf(t, "W5", 100), lf(t, "KK", 20), A("o2", 0, 20)
+
+        def raw(i):
+            return lh(t, "RAW", C * i + C, C * i)
+
+        def part(key, i, k=1):
+            return lf(t, key, 20 * (i + k), 20 * i)
+
         send_scales(t)
         send_codes(t, 1)
         for h in range(2):
@@ -308,18 +322,16 @@ def rank_program(g, core, T, topo):
         for h in range(2):
             a, z = CUT[h], CUT[h + 1]
             scalar1(lb(t, "F", z, a), A("ps%d" % (4 + h), 0, z - a), 0.0, ALU.is_gt)
-            if h == 0:
-                act(lb(t, "F2", z, a), lb(t, "F", z, a))
-            else:
-                scalar1(lb(t, "F2", z, a), A("ps%d" % (4 + h), 0, z - a), 0.0, ALU.is_gt)
-        two_at(M, F, A("nx16", 0, 20), F2, ALU.is_lt)
+            act(lb(t, "F2", z, a), lb(t, "F", z, a))
+        for h in range(2):
+            a, z = CUT[h], CUT[h + 1]
+            two_at(lb(t, "M", z, a), F, A("nx16", a // 16, z // 16), lb(t, "F2", z, a), ALU.is_lt)
 
         def own(b):
             act(A(n("tp"), TW * b, TW * b + C), A("ps%d" % b, 0, C))
 
         own(0)
-        own(1)
-        prefix(Cn, M)
+        scan(Cn, M, M, ALU.add, ALU.max)
         sl = A(n("sl"), 0, 12)
         for m in range(3):
             j, acc = lb(t, "JS", C * m + C, C * m), lf(t, "ACC", m + 1, m)
@@ -327,78 +339,75 @@ def rank_program(g, core, T, topo):
             op("s", lambda q, j=j, acc=acc, kb=kb: q.activation(j[0], Cn[0], ACT.Sign, bias=kb[0], scale=-1.0, accum_out=acc[0]),
                [j, acc], [Cn, kb])
         for m in (3, 4):
-            scalar1(lb(t, "JV", C * (m - 3) + C, C * (m - 3)), Cn, A("jw", m, m + 1), ALU.is_le)
+            scalar1(A("jv", AW * (m - 3), AW * (m - 3) + C), Cn, A("jw", m, m + 1), ALU.is_le, 2.0, ALU.mult)
         for m in (3, 4):
-            j, acc = lb(t, "JV", C * (m - 3) + C, C * (m - 3)), lf(t, "ACC", m + 1, m)
+            j, acc = A("jv", AW * (m - 3), AW * (m - 3) + C + 1), lf(t, "ACC", m + 1, m)
             op("v", lambda q, j=j, acc=acc: q.tensor_reduce(acc[0], j[0], AxisListType.X, ALU.add), [acc], [j])
-        copy(A(n("sl"), 3, 5), lf(t, "ACC", 5, 3))
-        if t == 0:
-            two(A("dmask", 0, C), A("m0", 0, C), A("m1", 0, C), ALU.add)
-        scalar1(A(n("sl"), 0, 3), lf(t, "ACC", 3), 0.5, ALU.mult, C / 2.0, ALU.add)
+        scalar1(A(n("sl"), 0, 5), lf(t, "ACC", 5), 0.5, ALU.mult, C / 2.0, ALU.add)
         pick("v", lh(t, "NXA", K), A("nxf", 0, AW), A(n("sl"), 0, 5))
-        scalar1(A(n("sl"), 10, 12), lb(t, "C", C, C - 2), float(K), ALU.min)
+        scalar1(A(n("sl"), 10, 12), lb(t, "C", C, C - 2), float(K), ALU.min, 2.0, ALU.mult)
         diagonal(lh(t, "NXR", K), lh(t, "NXA", K), K)
         scalar1(A(n("sl"), 5, 10), lh(t, "NXR", K, 15, 16), offp, ALU.subtract)
         send(A(n("ll"), 0, 12)[0], sl[0], n("rl"), where, [sl], n_out)
+        if t == 0:
+            for b in range(4):
+                iota_f(A("ta", AW * b + C, AW * b + AW), 0, AW - C, 0)
+            iota_f(A("wd", 0, 176), 0, 176, 0)
+            iota_f(A("o2", 0, 40), 0, 40, 0)
 
+        own(1)
         own(2)
         own(3)
         if t == 0:
-            for r in range(R):
-                for b in range(4):
-                    fill(A("ta%d" % r, AW * b + C, AW * b + AW), 0.0)
-                fill(lb(r, "WD", 176), 0.0)
-                fill(lf(r, "O2", 40), 0.0)
-            pf, io, nx16 = A("pvf", 0, C), A("iotaf", 0, C), A("nx16", 0, 20)
+            pf, io = A("pvf", 0, C), A("iotaf", 0, C)
             op("v", lambda q: q.tensor_copy(pf[0].indirect(nx16[0]), io[0]), [pf], [io, nx16])
-            copy(A("nxw", 0, 20), A("nxi", 0, 20))
-        two_at(B, F, A("nx16", 0, 20), F2, ALU.is_gt)
+        two_at(B, F, nx16, F2, ALU.is_gt)
         if t == 0:
             diagonal(A("pvr", 0, C), pf, C)
-        prefix(lb(t, "CB", C), B)
+        scan(CB, B, B, ALU.add, ALU.add)
         if t == 0:
-            scalar1(A("pv16", 0, 20), A("pvr", 15, C, 16), offp, ALU.subtract)
-            scalar1(A("pvw", 0, 20), A("pvr", 15, C, 16), offp, ALU.subtract)
-        diagonal(lh(t, "FR", C), F, C)
-        two(lb(t, "BR", C), B, lb(t, "CB", C), ALU.mult)
-        act(lb(t, "BR2", C), lb(t, "BR", C))
+            scalar1(pv16, A("pvr", 15, C, 16), offp, ALU.subtract)
+            scalar1(pvw, A("pvr", 15, C, 16), offp, ALU.subtract)
+        diagonal(raw(4), F, C)
+        pick("s", I, B, pv16)
+        pick("s", CBP, CB, pv16)
+        diagonal(raw(2), B, C)
+        diagonal(raw(0), CB, C)
         if t == 0:
-            two(A("dpn", 0, 20), A("pvw", 0, 20), A("nxw", 0, 20), ALU.subtract)
-        scalar1(lf(t, "FW", 20), lh(t, "FR", C, 15, 16), offp, ALU.subtract)
-        two(lf(t, "T1", 20), lf(t, "FW", 20), A("dpn", 0, 20), ALU.mult)
-        two(lf(t, "O", 20), lf(t, "T1", 20), A("nxw", 0, 20), ALU.add)
-        scalar1(lf(t, "T5", 20), lf(t, "FW", 20), float(K), ALU.mult)
-        two(lf(t, "T2", 20), A("jw", 0, 20), lf(t, "O", 20), ALU.subtract)
-        two_at(lb(t, "K", C), lb(t, "BR", C), A("pv16", 0, 20), lb(t, "BR2", C), ALU.add)
-        diagonal(lh(t, "KR", C), lb(t, "K", C), C)
-        KW = lf(t, "KW", 20)
-        scalar1(KW, lh(t, "KR", C, 15, 16), offp, ALU.subtract)
-        scalar1(lf(t, "Z", 20), KW, 0.5, ALU.is_gt)
-        scalar1(lf(t, "T6", 20), KW, 0.5, ALU.is_lt, 1000.0, ALU.mult)
-        scalar1(lf(t, "HU", 20), KW, 2.0, ALU.mult, C - 2.0, ALU.add)
-        two(lf(t, "T3", 20), lf(t, "T2", 20), lf(t, "Z", 20), ALU.mult)
+            two(A("cj", 0, 20), jw, nxw, ALU.subtract)
+            two(A("cj", 20, 40), jw, pvw, ALU.subtract)
+            two(A("cj", 40, 60), pvw, nxw, ALU.subtract)
+        diagonal(raw(3), I, C)
+        diagonal(raw(1), CBP, C)
+        scalar1(W5, lh(t, "RAW", 5 * C, 15, 16), offp, ALU.subtract)
+        two(lf(t, "PR", 40), part("W5", 0, 2), part("W5", 2, 2), ALU.mult)
+        two(lf(t, "X60", 60), part("W5", 2, 3), A("cj", 0, 60), ALU.mult)
+        two(lf(t, "Z", 20), part("W5", 2), part("W5", 3), ALU.add)
+        two(KK, part("PR", 0), part("PR", 1), ALU.add)
+        two(part("KK", 1), part("PR", 0), part("PR", 1), ALU.add)
+        two(lf(t, "ZC", 20), lf(t, "Z", 20), A("cz", 0, 20), ALU.mult)
+        two(lf(t, "Y", 20), part("X60", 0), part("X60", 1), ALU.add)
+        two(lf(t, "Y2", 20), part("X60", 2), nxw, ALU.add)
+        two(part("DT", 1), KK, part("W5", 2), ALU.subtract)
+        two(part("DT", 0), KK, lf(t, "ZC", 20), ALU.add)
+        two(O2, lf(t, "Y", 20), lf(t, "Y2", 20), ALU.add)
 
         for h in range(2):
             a, z = CUT[h], CUT[h + 1]
             for b in range(4):
                 bank = b if h else 4 + b
                 mm(bank, E(b), A(n("lc"), a, z), A(n("ls"), a, z), z - a)
-                act(A(n("ta"), AW * b + a, AW * b + z), A("ps%d" % bank, 0, z - a))
+                act(A("ta", AW * b + a, AW * b + z), A("ps%d" % bank, 0, z - a))
         for b in range(4):
-            pick("vvss"[b], A(n("at"), b, 4 * P2, 4), A(n("ta"), AW * b, AW * b + AW), A(n("ll"), 0, 10))
+            pick("vvss"[b], A(n("at"), b, 4 * P2, 4), A("ta", AW * b, AW * b + AW), A(n("ll"), 0, 10))
         ac, as_ = A(n("ac"), 0, P2), A(n("as"), 0, P2)
         quant(ac, as_, A(n("at"), 0, 4 * P2))
         for b in range(4):
             mm(b, W(b), ac, as_, P2)
         copy(lf(t, "NP", 2), A(n("ll"), 10, 12))
-        two(lf(t, "KK", 20), lf(t, "T6", 20), KW, ALU.add)
-        two(lf(t, "KK", 40, 20), lf(t, "T6", 20), KW, ALU.add)
-        two(lf(t, "O2", 20), lf(t, "O", 20), lf(t, "T3", 20), ALU.add)
         scalar1(lf(t, "U", 40), lf(t, "KK", 40), lf(t, "NP", 2, 1), ALU.is_le)
-        two(lf(t, "DT", 40, 20), lf(t, "T5", 20), KW, ALU.add)
-        two(lf(t, "DT", 20), lf(t, "HU", 20), lf(t, "O2", 20), ALU.subtract)
         two(lf(t, "MM", 40), lf(t, "U", 40), lf(t, "DT", 40), ALU.mult)
-        two(lf(t, "RR", 40), lf(t, "MM", 40), lf(t, "O2", 40), ALU.add)
+        two(lf(t, "RR", 40), lf(t, "MM", 40), A("o2", 0, 40), ALU.add)
         copy(A(n("hk"), 0, 40), lf(t, "RR", 40))
         for b in range(4):
             out, z = A(n("ht"), b, 4 * P2, 4), A("ps%d" % b, 0, P2)
@@ -418,32 +427,34 @@ def rank_program(g, core, T, topo):
                     act(out, z, 0.03125)
                 else:
                     scalar1(out, z, 0.03125, ALU.mult)
-        if t == 1:
-            quant(A("vc", 0, 128), A("vs", 0, 128), A("vt", 0, 512))
         act(lf(t, "PS", K), A("ps6", 0, K))
-        two(lb(t, "WD", K + 1, 1), lf(t, "PS", K), A("ps6", K, P2), ALU.is_lt)
-        two(lb(t, "WD", P2 + 1, K + 1), lf(t, "PS", K), A("ps6", K, P2), ALU.is_ge)
-        two_at(lh(t, "V", C), lb(t, "WD", 176), A(n("hk"), 20, 40), hb, ALU.add)
+        two(A("wd", 1, P2 + 1, 2), lf(t, "PS", K), A("ps6", K, P2), ALU.is_lt)
+        two(A("wd", 2, P2 + 1, 2), lf(t, "PS", K), A("ps6", K, P2), ALU.is_ge)
+        two_at(lh(t, "V", C), A("wd", 0, 176), A(n("hk"), 20, 40), hb, ALU.add)
         diagonal(lh(t, "VR", C), lh(t, "V", C), C)
         scalar1(A(n("h"), 0, 20), lh(t, "VR", C, 15, 16), offp, ALU.subtract)
         for h in range(2):
             a, z = CUT[h], CUT[h + 1]
             for b in range(4):
-                pick("vvss"[b], A("x%d" % (t + 1), 4 * a + b, 4 * z, 4), A(n("tp"), TW * b, TW * b + TW),
+                pick(("vvss", "vsss")[h][b], A("x%d" % (t + 1), 4 * a + b, 4 * z, 4), A(n("tp"), TW * b, TW * b + TW),
                      A(n("h"), a // 16, z // 16))
             state_codes(t + 1, h)
             if h == 0 and t + 1 < R:
                 send_codes(t + 1, 0)
+            if h == 0 and t + 1 == R:
+                quant(A("vc", 0, 128), A("vs", 0, 128), A("vt", 0, 512))
+                dma("y", T.oc[:, 0:4 * z], U8(A("qc3", 0, z)), [], [A("qc3", 0, z)])
 
     for h in range(2):
         a, z = CUT[h], CUT[h + 1]
         mm(4 + h, (A("vc", 0, 128), A("vs", 0, 128)), A("qc3", a, z), A("qs3", a, z), z - a)
-    dma("y", T.oc[:, :], U8(A("qc3", 0, C)), [], [A("qc3", 0, C)])
+    copy(A("ott", 0, C), lh(R - 1, "V", C))
+    act(A("yt", 0, CUT[1]), A("ps4", 0, CUT[1]))
+    dma("s", T.y[:, 0:CUT[1]], A("yt", 0, CUT[1])[0], [], [A("yt", 0, CUT[1])])
+    dma("y", T.oc[:, 4 * CUT[1]:4 * C], U8(A("qc3", CUT[1], C)), [], [A("qc3", CUT[1], C)])
     for k in range(4):
         dma("y", T.osc[4 * k:4 * k + 4, :], T.qs3[32 * k:32 * k + 4, 0:C], [], [A("qs3", 0, C)])
-    act(A("yt", 0, CUT[1]), A("ps4", 0, CUT[1]))
-    copy(A("yt", CUT[1], C), A("ps5", 0, C - CUT[1]))
-    dma("s", T.y[:, :], A("yt", 0, C)[0], [], [A("yt", 0, C)])
-    copy(A("ott", 0, C), lh(R - 1, "V", C))
+    act(A("yt", CUT[1], C), A("ps5", 0, C - CUT[1]))
+    dma("s", T.y[:, CUT[1]:C], A("yt", CUT[1], C)[0], [], [A("yt", CUT[1], C)])
     dma("y", T.ot[:, :], T.ott[0:128:16, 0:C], [], [A("ott", 0, C)])
     close()

import numpy as np
from concourse.mybir import dt, AluOpType, AxisListType, ActivationFunctionType

ALU = AluOpType
ACT = ActivationFunctionType
C, K, R, N = 320, 80, 3, 4
CUT = (0, 192, C)
P2 = 2 * K
TW = C + P2
AW = C + 16
OFF, BIG = 1024.0, 4096.0
HALF = "float16"


def _layout(sizes, align):
    at, pos = {}, 0
    for name, n in sizes:
        at[name] = pos
        pos += -(-n // align) * align
    return at, pos


LB, LBW = _layout([("F", C), ("F2", C), ("M", C), ("C", C), ("B", C), ("CB", C), ("CBP", C), ("I", C), ("JS", 3 * C)], 16)
LH, LHW = _layout([("NXA", K), ("NXR", K), ("RAW", 5 * C), ("V", C), ("VR", C)], 16)
LF, LFW = _layout([("HB", C), ("ACC", 8), ("PS", K), ("W5", 100), ("PR", 40), ("KK", 40), ("X60", 60), ("Y", 20), ("Y2", 20),
                   ("Z", 20), ("ZC", 20), ("DT", 40), ("U", 40), ("MM", 40), ("RR", 40), ("NP", 2)], 8)

X4 = "float8_e4m3fn_x4"
SCRATCH = {
    "iotaf": ("sbuf", [128, TW], "float32"), "mi": ("sbuf", [128, 16], "int32"), "mj": ("sbuf", [128, 16], "int32"),
    "m0": ("sbuf", [128, 16], HALF), "m1": ("sbuf", [128, 16], HALF), "dmask": ("sbuf", [128, C], HALF),
    "pi": ("sbuf", [128, 20], "int32"), "pj": ("sbuf", [128, 20], "int32"), "j0": ("sbuf", [128, 20], "int32"),
    "jw": ("sbuf", [128, 20], "float32"), "offp": ("sbuf", [128, 2], "float32"), "kb": ("sbuf", [128, 8], "float32"),
    "uli": ("sbuf", [128, 8], "int32"), "ul": ("sbuf", [128, 8], "uint16"),
    "ones": ("sbuf", [128, 128], "bfloat16"), "eb": ("sbuf", [128, 516], "bfloat16"),
    "ec": ("sbuf", [128, 512], X4), "es": ("sbuf", [128, 512], "uint8"),
    "ut": ("sbuf", [128, 512], "bfloat16"), "uc": ("sbuf", [128, 128], X4), "us": ("sbuf", [128, 128], "uint8"),
    "upc": ("sbuf", [128, 128], X4), "ups": ("sbuf", [128, 128], "uint8"),
    "vt": ("sbuf", [128, 512], "bfloat16"), "vc": ("sbuf", [128, 128], X4), "vs": ("sbuf", [128, 128], "uint8"),
    "lwc": ("sbuf", [128, 512], X4), "lws": ("sbuf", [128, 512], "uint8"),
    "nxi": ("sbuf", [128, 20], "int32"), "nx16": ("sbuf", [128, 20], "uint16"), "nxw": ("sbuf", [128, 20], "float32"),
    "nxf": ("sbuf", [128, AW], "float32"), "pvf": ("sbuf", [128, C], "float32"), "pvr": ("sbuf", [128, C], "float32"),
    "pvw": ("sbuf", [128, 20], "float32"), "pv16": ("sbuf", [128, 20], "uint16"), "cj": ("sbuf", [128, 60], "float32"),
    "cz": ("sbuf", [128, 20], "float32"),
    "ta": ("sbuf", [128, 4 * AW], "bfloat16"), "wd": ("sbuf", [128, 176], "bfloat16"),
    "jv": ("sbuf", [128, 2 * AW], "bfloat16"), "o2": ("sbuf", [128, 40], "float32"),
    "lb": ("sbuf", [128, R * LBW], "bfloat16"), "lf": ("sbuf", [128, R * LFW], "float32"), "lh": ("sbuf", [128, R * LHW], HALF),
    "yt": ("sbuf", [128, C], "float32"), "ott": ("sbuf", [128, C], "float32"),
}
for _t in range(R + 1):
    SCRATCH["x%d" % _t] = ("sbuf", [128, 4 * C], "bfloat16")
    SCRATCH["qc%d" % _t] = ("sbuf", [128, C], X4)
    SCRATCH["qs%d" % _t] = ("sbuf", [128, C], "uint8")
for _t in range(R):
    SCRATCH["tp%d" % _t] = ("sbuf", [128, 4 * TW], "bfloat16")
    SCRATCH["lc%d" % _t] = ("sbuf", [128, C], X4)
    SCRATCH["ls%d" % _t] = ("sbuf", [128, C], "uint8")
    SCRATCH["at%d" % _t] = ("sbuf", [128, 4 * P2], "bfloat16")
    SCRATCH["ac%d" % _t] = ("sbuf", [128, P2], X4)
    SCRATCH["as%d" % _t] = ("sbuf", [128, P2], "uint8")
    SCRATCH["ht%d" % _t] = ("sbuf", [128, 4 * P2], "bfloat16")
    SCRATCH["hc%d" % _t] = ("sbuf", [128, P2], X4)
    SCRATCH["hs%d" % _t] = ("sbuf", [128, P2], "uint8")
    SCRATCH["sl%d" % _t] = ("sbuf", [128, 12], "uint16")
    SCRATCH["ll%d" % _t] = ("sbuf", [128, 12], "uint16")
    SCRATCH["hk%d" % _t] = ("sbuf", [128, 40], "uint16")
    SCRATCH["h%d" % _t] = ("sbuf", [128, 20], "uint16")
for _b in range(8):
    SCRATCH["ps%d" % _b] = ("psum", [128, 512], "float32")

SEMAPHORES = (["cv", "cs", "ct", "cg", "loc"] + ["d%d" % i for i in range(20)]
              + [s + "%d" % t for t in range(R) for s in ("ra", "rb", "rs", "rl")])


def _cols(a, b, step=1):
    m = 0
    for c in range(a, b, step):
        m |= 1 << c
    return m


def _machine(g, T):
    queues = {"v": g.vector, "s": g.scalar, "t": g.tensor, "g": g, "y": g.sync}
    total, clock, hist, fresh = {}, {}, {}, [0]
    known = dict((q, {}) for q in queues)

    def wait(q, sem, val):
        if known[q].get(sem, 0) >= val:
            return
        queues[q].wait_ge(T.sem[sem], val)
        for s, n in clock.get((sem, val), {}).items():
            known[q][s] = max(known[q].get(s, 0), n)
        known[q][sem] = max(known[q].get(sem, 0), val)

    def order(q, writes, reads):
        need = {}
        for acc, wr in [(a, True) for a in writes] + [(a, False) for a in reads]:
            for mask, oq, sem, val, owr in hist.get(acc[1], []):
                if not mask & acc[2]:
                    continue
                if wr and not owr and oq == q:
                    continue
                if not wr and not owr and (oq == q or not acc[1].startswith("ps")):
                    continue
                need[sem] = max(need.get(sem, 0), val)
        need = [(s, n) for s, n in need.items() if known[q].get(s, 0) < n]
        for s, n in need:
            if not any(clock.get(o, {}).get(s, 0) >= n for o in need if o != (s, n)):
                wait(q, s, n)

    def note(q, sem, val, writes, reads):
        for a in writes:
            hist.setdefault(a[1], []).append((a[2], q, sem, val, True))
        for a in reads:
            hist.setdefault(a[1], []).append((a[2], q, sem, val, False))

    def op(q, call, writes, reads):
        order(q, writes, reads)
        sem = "c" + q
        val = total[sem] = total.get(sem, 0) + 1
        call(queues[q]).then_inc(T.sem[sem], 1)
        clock[(sem, val)] = dict(known[q])
        note(q, sem, val, writes, reads)

    def dma(q, out, in_, writes, reads):
        order(q, writes, reads)
        sem = "d%d" % fresh[0]
        fresh[0] += 1
        total[sem] = 16
        queues[q].dma_start(out, in_).then_inc(T.sem[sem], 16)
        clock[(sem, 16)] = dict(known[q])
        note("d", sem, 16, writes, reads)

    def send(out, in_, rsem, where, reads, engines):
        order("g", [], reads)
        total["loc"] = total.get("loc", 0) + engines
        g.remote_dma(out, in_, T.sem[rsem], T.sem.loc, where[0], where[1], where[2])

    def lands(writes, rsem, engines):
        total[rsem] = engines
        note("net", rsem, engines, writes, [])

    def close():
        for sem in sorted(total):
            wait("g", sem, total[sem])

    return op, dma, send, lands, close


def rank_program(g, core, T, topo):
    rank = T.rank_of(core)
    if rank is None:
        return
    op, dma, send, lands, close = _machine(g, T)
    dst, src = T.cores[(rank + 1) % N], T.cores[rank - 1]
    rid, pid = topo.addr(dst)[:2]
    where = (pid, rid, topo.mask(core, dst))
    n_out, n_in = len(topo.engines(core, dst)), len(topo.engines(src, core))

    def A(name, a, b, step=1):
        return (T[name][:, a:b:step] if step > 1 else T[name][:, a:b], name, _cols(a, b, step))

    def lb(t, key, n, a=0, step=1):
        o = t * LBW + LB[key]
        return A("lb", o + a, o + n, step)

    def lf(t, key, n, a=0, step=1):
        o = t * LFW + LF[key]
        return A("lf", o + a, o + n, step)

    def lh(t, key, n, a=0, step=1):
        o = t * LHW + LH[key]
        return A("lh", o + a, o + n, step)

    def U8(acc):
        return acc[0].bitcast(dt.uint8)

    def E(b):
        return A("ec", 128 * b, 128 * b + 128), A("es", 128 * b, 128 * b + 128)

    def W(b):
        return A("lwc", 128 * b, 128 * b + 128), A("lws", 128 * b, 128 * b + 128)

    def fill(out, value):
        op("v", lambda q: q.memset(out[0], value), [out], [])

    def copy(out, in_):
        op("v", lambda q: q.tensor_copy(out[0], in_[0]), [out], [in_])

    def pick(q, out, win, off):
        if q == "v":
            op("v", lambda e: e.tensor_copy(out[0], win[0].indirect(off[0])), [out], [win, off])
        else:
            op("s", lambda e: e.activation(out[0], win[0].indirect(off[0]), ACT.Copy), [out], [win, off])

    def scalar1(out, in0, s1, op0, s2=None, op1=None):
        reads = [in0] + ([s1] if isinstance(s1, tuple) else [])
        a1 = s1[0] if isinstance(s1, tuple) else s1
        if op1 is None:
            op("v", lambda q: q.tensor_scalar(out[0], in0[0], a1, None, op0), [out], reads)
        else:
            op("v", lambda q: q.tensor_scalar(out[0], in0[0], a1, s2, op0, op1), [out], reads)

    def two(out, in0, in1, o):
        op("v", lambda q: q.tensor_tensor(out[0], in0[0], in1[0], o), [out], [in0, in1])

    def two_at(out, win, off, in1, o):
        op("v", lambda q: q.tensor_tensor(out[0], win[0].indirect(off[0]), in1[0], o), [out], [win, off, in1])

    def scan(out, d0, d1, op0, op1):
        op("v", lambda q: q.tensor_tensor_scan(out[0], d0[0], d1[0], 0.0, op0, op1), [out], [d0, d1])

    def diagonal(raw, rows, n):
        scan(raw, A("dmask", 0, n), rows, ALU.add, ALU.max)

    def quant(c, s, tile):
        op("v", lambda q: q.quantize_mx(c[0], s[0], tile[0]), [c, s], [tile])

    def mm(bank, w, xc, xs, n):
        out = A("ps%d" % bank, 0, n)
        op("t", lambda q: q.matmul_mx(out[0], w[0][0], w[1][0], xc[0], xs[0], True, True), [out], [w[0], w[1], xc, xs])

    def act(out, in_, scale=None):
        if scale is None:
            op("s", lambda q: q.activation(out[0], in_[0], ACT.Copy), [out], [in_])
        else:
            op("s", lambda q: q.activation(out[0], in_[0], ACT.Copy, scale=scale), [out], [in_])

    def load(q, name, a, b, ap):
        w = A(name, a, b)
        dma(q, w[0], ap, [w], [])

    def iota(out, pattern, base, ch):
        op("g", lambda q: q.iota(out[0], pattern, base, ch), [out], [])

    def iota_f(out, step, n, base):
        op("g", lambda q: q.iota(out[0], [[step, n]], base, 0, allow_small_or_imprecise_dtypes=True), [out], [])

    def state_codes(t, h):
        a, b = CUT[h], CUT[h + 1]
        quant(A("qc%d" % t, a, b), A("qs%d" % t, a, b), A("x%d" % t, 4 * a, 4 * b))

    def send_codes(t, h):
        i = A("qc%d" % t, CUT[h], CUT[h + 1])
        send(U8(A("lc%d" % t, CUT[h], CUT[h + 1])), U8(i), ("ra%d", "rb%d")[h] % t, where, [i], n_out)

    def send_scales(t):
        i = A("qs%d" % t, 0, C)
        send(A("ls%d" % t, 0, C)[0], i[0], "rs%d" % t, where, [i], n_out)

    load("y", "nxi", 0, 20, T.nx[:, :])
    load("s", "ut", 0, 512, T.u[:, :])
    load("y", "x0", 0, 4 * CUT[1], T.x[:, 0:4 * CUT[1]])
    load("y", "x0", 4 * CUT[1], 4 * C, T.x[:, 4 * CUT[1]:4 * C])
    w = A("lwc", 0, 512)
    dma("y", U8(w), T.wc[:, :], [w], [])
    load("s", "lws", 0, 512, T.ws[:, :])
    load("y", "vt", 0, 512, T.v[:, :])
    for t in range(R):
        lands([A("lc%d" % t, 0, CUT[1])], "ra%d" % t, n_in)
        lands([A("lc%d" % t, CUT[1], C)], "rb%d" % t, n_in)
        lands([A("ls%d" % t, 0, C)], "rs%d" % t, n_in)
        lands([A("ll%d" % t, 0, 12)], "rl%d" % t, n_in)

    fill(A("ones", 0, 128), 1.0)
    fill(A("eb", 0, 516), 0.0)
    iota(A("uli", 0, 8), [[16, 8]], 0, 0)
    iota(A("mi", 0, 16), [[1, 16]], 128, -1)
    iota(A("pi", 0, 20), [[0, 20]], 0, 1)
    iota(A("j0", 0, 20), [[16, 20]], 0, 0)
    e, o = A("eb", 3, 515, 4), A("ones", 0, 128)
    op("g", lambda q: q.affine_select(e[0], o[0], [[-1, 128]], ALU.is_equal, 0.0, 0, 1), [e], [o])
    iota_f(A("iotaf", 0, TW), 1, TW, 0)
    for b in range(2):
        iota_f(A("jv", AW * b + C, AW * b + C + 8), 0, 8, -C)
    copy(A("ul", 0, 8), A("uli", 0, 8))
    scalar1(A("mj", 0, 16), A("mi", 0, 16), 15, ALU.bitwise_and)
    scalar1(A("pj", 0, 20), A("pi", 0, 20), 15, ALU.bitwise_and)
    scalar1(A("m0", 0, 16), A("mj", 0, 16), 0.0, ALU.is_equal, -BIG, ALU.mult)
    scalar1(A("m1", 0, 16), A("mj", 0, 16), 1.0, ALU.is_equal, OFF, ALU.mult)
    two(A("jw", 0, 20), A("j0", 0, 20), A("pj", 0, 20), ALU.add)
    two(A("dmask", 0, 16), A("m0", 0, 16), A("m1", 0, 16), ALU.add)
    scalar1(A("offp", 0, 2), A("pj", 0, 2), 14.5, ALU.is_lt, OFF, ALU.mult)
    for b in range(4):
        quant(E(b)[0], E(b)[1], A("eb", 3 - b, 515 - b))
        copy(A("dmask", 16 << b, 32 << b), A("dmask", 0, 16 << b))
    fill(A("nxf", C, AW), float(C))
    copy(A("dmask", 256, C), A("dmask", 0, C - 256))
    scalar1(A("kb", 0, 5), A("jw", 0, 5), 0.5, ALU.add)
    copy(A("nx16", 0, 20), A("nxi", 0, 20))
    copy(A("nxw", 0, 20), A("nxi", 0, 20))
    scalar1(A("cz", 0, 20), A("jw", 0, 20), -1.0, ALU.mult, C - 2.0, ALU.add)
    quant(A("uc", 0, 128), A("us", 0, 128), A("ut", 0, 512))
    up, ic_, ul = (A("upc", 0, 128), A("ups", 0, 128)), A("uc", 0, 128), A("ul", 0, 8)
    op("v", lambda q: q.tensor_copy(up[0][0].bitcast(dt.uint32), ic_[0].bitcast(dt.uint32).indirect(ul[0])), [up[0]], [ic_, ul])
    pick("s", up[1], A("us", 0, 128), ul)
    state_codes(0, 0)
    send_codes(0, 0)
    state_codes(0, 1)
    pick("s", A("nxf", 0, C), A("iotaf", 0, C), A("nx16", 0, 20))
    offp, nx16, pv16, nxw, jw, pvw = A("offp", 0, 1), A("nx16", 0, 20), A("pv16", 0, 20), A("nxw", 0, 20), A("jw", 0, 20), A("pvw", 0, 20)

    for t in range(R):
        n = lambda s: "%s%d" % (s, t)
        qc, qs = A(n("qc"), 0, C), A(n("qs"), 0, C)
        F, F2, M, Cn, B = lb(t, "F", C), lb(t, "F2", C), lb(t, "M", C), lb(t, "C", C), lb(t, "B", C)
        CB, CBP, I, W5, KK, O2 = lb(t, "CB", C), lb(t, "CBP", C), lb(t, "I", C), lf(t, "W5", 100), lf(t, "KK", 20), A("o2", 0, 20)

        def raw(i):
            return lh(t, "RAW", C * i + C, C * i)

        def part(key, i, k=1):
            return lf(t, key, 20 * (i + k), 20 * i)

        send_scales(t)
        send_codes(t, 1)
        for h in range(2):
            a, z = CUT[h], CUT[h + 1]
            mm(4 + h, up, A(n("qc"), a, z), A(n("qs"), a, z), z - a)
        for b in range(4):
            mm(b, E(b), qc, qs, C)
        for h in range(2):
            a, z = CUT[h], CUT[h + 1]
            scalar1(lb(t, "F", z, a), A("ps%d" % (4 + h), 0, z - a), 0.0, ALU.is_gt)
            act(lb(t, "F2", z, a), lb(t, "F", z, a))
        for h in range(2):
            a, z = CUT[h], CUT[h + 1]
            two_at(lb(t, "M", z, a), F, A("nx16", a // 16, z // 16), lb(t, "F2", z, a), ALU.is_lt)

        def own(b):
            act(A(n("tp"), TW * b, TW * b + C), A("ps%d" % b, 0, C))

        own(0)
        scan(Cn, M, M, ALU.add, ALU.max)
        sl = A(n("sl"), 0, 12)
        for m in range(3):
            j, acc = lb(t, "JS", C * m + C, C * m), lf(t, "ACC", m + 1, m)
            kb = A("kb", m, m + 1)
            op("s", lambda q, j=j, acc=acc, kb=kb: q.activation(j[0], Cn[0], ACT.Sign, bias=kb[0], scale=-1.0, accum_out=acc[0]),
               [j, acc], [Cn, kb])
        for m in (3, 4):
            scalar1(A("jv", AW * (m - 3), AW * (m - 3) + C), Cn, A("jw", m, m + 1), ALU.is_le, 2.0, ALU.mult)
        for m in (3, 4):
            j, acc = A("jv", AW * (m - 3), AW * (m - 3) + C + 1), lf(t, "ACC", m + 1, m)
            op("v", lambda q, j=j, acc=acc: q.tensor_reduce(acc[0], j[0], AxisListType.X, ALU.add), [acc], [j])
        scalar1(A(n("sl"), 0, 5), lf(t, "ACC", 5), 0.5, ALU.mult, C / 2.0, ALU.add)
        pick("v", lh(t, "NXA", K), A("nxf", 0, AW), A(n("sl"), 0, 5))
        scalar1(A(n("sl"), 10, 12), lb(t, "C", C, C - 2), float(K), ALU.min, 2.0, ALU.mult)
        diagonal(lh(t, "NXR", K), lh(t, "NXA", K), K)
        scalar1(A(n("sl"), 5, 10), lh(t, "NXR", K, 15, 16), offp, ALU.subtract)
        send(A(n("ll"), 0, 12)[0], sl[0], n("rl"), where, [sl], n_out)
        if t == 0:
            for b in range(4):
                iota_f(A("ta", AW * b + C, AW * b + AW), 0, AW - C, 0)
            iota_f(A("wd", 0, 176), 0, 176, 0)
            iota_f(A("o2", 0, 40), 0, 40, 0)

        own(1)
        own(2)
        own(3)
        if t == 0:
            pf, io = A("pvf", 0, C), A("iotaf", 0, C)
            op("v", lambda q: q.tensor_copy(pf[0].indirect(nx16[0]), io[0]), [pf], [io, nx16])
        two_at(B, F, nx16, F2, ALU.is_gt)
        if t == 0:
            diagonal(A("pvr", 0, C), pf, C)
        scan(CB, B, B, ALU.add, ALU.add)
        if t == 0:
            scalar1(pv16, A("pvr", 15, C, 16), offp, ALU.subtract)
            scalar1(pvw, A("pvr", 15, C, 16), offp, ALU.subtract)
        diagonal(raw(4), F, C)
        pick("s", I, B, pv16)
        pick("s", CBP, CB, pv16)
        diagonal(raw(2), B, C)
        diagonal(raw(0), CB, C)
        if t == 0:
            two(A("cj", 0, 20), jw, nxw, ALU.subtract)
            two(A("cj", 20, 40), jw, pvw, ALU.subtract)
            two(A("cj", 40, 60), pvw, nxw, ALU.subtract)
        diagonal(raw(3), I, C)
        diagonal(raw(1), CBP, C)
        scalar1(W5, lh(t, "RAW", 5 * C, 15, 16), offp, ALU.subtract)
        two(lf(t, "PR", 40), part("W5", 0, 2), part("W5", 2, 2), ALU.mult)
        two(lf(t, "X60", 60), part("W5", 2, 3), A("cj", 0, 60), ALU.mult)
        two(lf(t, "Z", 20), part("W5", 2), part("W5", 3), ALU.add)
        two(KK, part("PR", 0), part("PR", 1), ALU.add)
        two(part("KK", 1), part("PR", 0), part("PR", 1), ALU.add)
        two(lf(t, "ZC", 20), lf(t, "Z", 20), A("cz", 0, 20), ALU.mult)
        two(lf(t, "Y", 20), part("X60", 0), part("X60", 1), ALU.add)
        two(lf(t, "Y2", 20), part("X60", 2), nxw, ALU.add)
        two(part("DT", 1), KK, part("W5", 2), ALU.subtract)
        two(part("DT", 0), KK, lf(t, "ZC", 20), ALU.add)
        two(O2, lf(t, "Y", 20), lf(t, "Y2", 20), ALU.add)

        for h in range(2):
            a, z = CUT[h], CUT[h + 1]
            for b in range(4):
                bank = b if h else 4 + b
                mm(bank, E(b), A(n("lc"), a, z), A(n("ls"), a, z), z - a)
                act(A("ta", AW * b + a, AW * b + z), A("ps%d" % bank, 0, z - a))
        for b in range(4):
            pick("vvss"[b], A(n("at"), b, 4 * P2, 4), A("ta", AW * b, AW * b + AW), A(n("ll"), 0, 10))
        ac, as_ = A(n("ac"), 0, P2), A(n("as"), 0, P2)
        quant(ac, as_, A(n("at"), 0, 4 * P2))
        for b in range(4):
            mm(b, W(b), ac, as_, P2)
        copy(lf(t, "NP", 2), A(n("ll"), 10, 12))
        scalar1(lf(t, "U", 40), lf(t, "KK", 40), lf(t, "NP", 2, 1), ALU.is_le)
        two(lf(t, "MM", 40), lf(t, "U", 40), lf(t, "DT", 40), ALU.mult)
        two(lf(t, "RR", 40), lf(t, "MM", 40), A("o2", 0, 40), ALU.add)
        copy(A(n("hk"), 0, 40), lf(t, "RR", 40))
        for b in range(4):
            out, z = A(n("ht"), b, 4 * P2, 4), A("ps%d" % b, 0, P2)
            if b < 2:
                act(out, z, 0.03125)
            else:
                scalar1(out, z, 0.03125, ALU.mult)
        hc, hs = A(n("hc"), 0, P2), A(n("hs"), 0, P2)
        quant(hc, hs, A(n("ht"), 0, 4 * P2))
        mm(6, up, hc, hs, P2)
        hb = lf(t, "HB", C)
        pick("s", hb, A("iotaf", 0, TW), A(n("hk"), 0, 20))
        for b in range(4):
            for i in range(2):
                out, z = A(n("tp"), TW * b + C + i, TW * b + TW, 2), A("ps%d" % b, K * i, K * i + K)
                if b < 2:
                    act(out, z, 0.03125)
                else:
                    scalar1(out, z, 0.03125, ALU.mult)
        act(lf(t, "PS", K), A("ps6", 0, K))
        two(A("wd", 1, P2 + 1, 2), lf(t, "PS", K), A("ps6", K, P2), ALU.is_lt)
        two(A("wd", 2, P2 + 1, 2), lf(t, "PS", K), A("ps6", K, P2), ALU.is_ge)
        two_at(lh(t, "V", C), A("wd", 0, 176), A(n("hk"), 20, 40), hb, ALU.add)
        diagonal(lh(t, "VR", C), lh(t, "V", C), C)
        scalar1(A(n("h"), 0, 20), lh(t, "VR", C, 15, 16), offp, ALU.subtract)
        for h in range(2):
            a, z = CUT[h], CUT[h + 1]
            for b in range(4):
                pick(("vvss", "vsss")[h][b], A("x%d" % (t + 1), 4 * a + b, 4 * z, 4), A(n("tp"), TW * b, TW * b + TW),
                     A(n("h"), a // 16, z // 16))
            state_codes(t + 1, h)
            if h == 0 and t + 1 < R:
                send_codes(t + 1, 0)
            if h == 0 and t + 1 == R:
                quant(A("vc", 0, 128), A("vs", 0, 128), A("vt", 0, 512))
                dma("y", T.oc[:, 0:4 * z], U8(A("qc3", 0, z)), [], [A("qc3", 0, z)])

    for h in range(2):
        a, z = CUT[h], CUT[h + 1]
        mm(4 + h, (A("vc", 0, 128), A("vs", 0, 128)), A("qc3", a, z), A("qs3", a, z), z - a)
    copy(A("ott", 0, C), lh(R - 1, "V", C))
    act(A("yt", 0, CUT[1]), A("ps4", 0, CUT[1]))
    dma("s", T.y[:, 0:CUT[1]], A("yt", 0, CUT[1])[0], [], [A("yt", 0, CUT[1])])
    dma("y", T.oc[:, 4 * CUT[1]:4 * C], U8(A("qc3", CUT[1], C)), [], [A("qc3", CUT[1], C)])
    for k in range(4):
        dma("y", T.osc[4 * k:4 * k + 4, :], T.qs3[32 * k:32 * k + 4, 0:C], [], [A("qs3", 0, C)])
    act(A("yt", CUT[1], C), A("ps5", 0, C - CUT[1]))
    dma("s", T.y[:, CUT[1]:C], A("yt", CUT[1], C)[0], [], [A("yt", CUT[1], C)])
    dma("y", T.ot[:, :], T.ott[0:128:16, 0:C], [], [A("ott", 0, C)])
    close()
